import numpy as np
import ml_dtypes


def mxq(x, axis, fmt="e4m3"):
    dtype, down = {"e4m3": (ml_dtypes.float8_e4m3fn, 7), "e5m2": (ml_dtypes.float8_e5m2, 14)}[fmt]
    v = np.moveaxis(np.asarray(x, np.float32).astype(ml_dtypes.bfloat16).astype(np.float64), axis, -1)
    blocks = v.reshape(v.shape[:-1] + (-1, 32))
    amax = np.abs(blocks).max(-1, keepdims=True)
    byte = np.maximum(np.where(amax > 0, np.frexp(amax)[1] - 1 + 127, 0) - down, 1)
    scale = np.exp2(byte - 127.0)
    codes = (blocks / scale).astype(np.float32).astype(dtype).astype(np.float64)
    return np.moveaxis((codes * scale).reshape(v.shape), -1, axis)


WIDE = False


def mx_kscale(k):
    if not WIDE:
        return np.ones(k)
    levels = np.array([10, -10, 5, -5, 0])
    if k % 512:
        return np.exp2(np.random.permutation(np.resize(levels, k // 32))).repeat(32)
    a = np.empty((k // 512, 16))
    for p in range(k // 512):
        a[p, :8] = np.random.permutation(np.resize(levels, 8))
        for g in range(8):
            far = levels[np.abs(levels - a[p, g]) >= 10]
            a[p, g + 8] = far[np.random.randint(len(far))]
    return np.exp2(a.ravel()).repeat(32)


BF16 = ml_dtypes.bfloat16


def bf(x):
    return np.asarray(x, np.float32).astype(BF16)


def f64(x):
    return np.asarray(x).astype(np.float64)

E4M3FN = np.array([(-1.0 if i & 128 else 1.0) * ((1.0 + (i & 7) / 8.0) * 2.0 ** (((i >> 3) & 15) - 7) if i & 120 else (i & 7) * 2.0 ** -9) for i in range(256)])


def e4m3fn_bytes(y):
    return np.clip(np.asarray(y, np.float64), -448.0, 448.0).astype(np.float32).astype(ml_dtypes.float8_e4m3fn).view(np.uint8)


def e4m3fn_values(b):
    return E4M3FN[b]

def planes(Y):
    n, m = Y.shape
    b = f64(bf(Y)).reshape(n // 32, 32, m)
    amax = np.abs(b).max(1)
    byte = np.clip(np.where(amax > 0, np.frexp(amax)[1] - 1 + 127 - 7, 1), 1, 254)
    codes = (b * np.exp2(127.0 - byte)[:, None, :]).reshape(n, m).astype(np.float32).astype(ml_dtypes.float8_e4m3fn).view(np.uint8)
    words = codes.reshape(n // 512, 128, 4, m).transpose(0, 1, 3, 2)
    return np.ascontiguousarray(words), np.ascontiguousarray(byte.astype(np.uint8).reshape(n // 512, 16, m))


T, K, N, G, P = 1024, 1536, 2048, 128, 64


def setup_inputs():
    s = mx_kscale(K)
    X = (np.random.randn(T, K) + 0.7 * np.random.randn(1, K)) * s
    X_mean = bf(X.mean(axis=0, keepdims=True))
    C = X - f64(X_mean)
    X_scale = (np.abs(C).reshape(T, K // G, G).max(axis=2) / 448.0).astype(np.float32)
    X_bytes = e4m3fn_bytes(C / np.repeat(f64(X_scale), G, axis=1))
    W = np.random.randn(K, N) / np.sqrt(K) / s[:, None]
    page = np.repeat(np.random.uniform(0.25, 1.0, N // P), P)
    place = np.exp(-0.8 * np.abs(np.random.randn(N)))
    return {
        "X_bytes": X_bytes,
        "X_scale": X_scale,
        "X_mean": X_mean,
        "W": bf(W),
        "user_bias": bf(0.5 * np.random.randn(T, 1)),
        "item_bias": bf(0.5 * np.random.randn(1, N)),
        "exam": bf((page * place).reshape(1, N)),
    }

def reference(X_bytes, X_scale, X_mean, W, user_bias, item_bias, exam):
    X = e4m3fn_values(X_bytes) * np.repeat(f64(X_scale), G, axis=1) + f64(X_mean)
    Z = mxq(X, 1, "e4m3") @ mxq(f64(W), 0, "e4m3")
    Z = Z + f64(user_bias) + f64(item_bias)
    y = f64(exam) * (1.0 / (1.0 + np.exp(-Z)))
    words, scales = planes(y.T)
    return y, words, scales

@@ -1,0 +1,484 @@
+from contextlib import ExitStack
+
+import concourse.mybir as mybir
+from concourse.masks import make_identity
+
+T, K, N = 1024, 1536, 2048
+FLOPS = 2 * T * K * N
+
+F32 = mybir.dt.float32
+BF16 = mybir.dt.bfloat16
+U32 = mybir.dt.uint32
+I32 = mybir.dt.int32
+U8 = mybir.dt.uint8
+FP8 = mybir.dt.float8_e4m3fn
+FP8X4 = mybir.dt.float8_e4m3fn_x4
+ALU = mybir.AluOpType
+ACT = mybir.ActivationFunctionType
+
+P = 128
+PASSES = 3
+GROUP = 512
+HALF = 1024
+TILES = 8
+BLOCK = 128
+BLOCKS = 12
+ACC_BANKS = 2
+TURN_BANKS = 4
+UNITS = [(0, 0), (1, 0), (0, 1), (1, 1)] + [(i, h) for i in range(2, TILES) for h in range(2)]
+
+
+def tile_centred_click_probability_b15_kernel(
+    tc, X_bytes, X_scale, X_mean, W, user_bias, item_bias, exam, out_0, out_1, out_2
+):
+    nc = tc.nc
+    words_out = out_1.bitcast(I32).rearrange("g p m o -> p g (m o)")
+    scales_out = out_2.bitcast(I32)
+
+    with ExitStack() as ctx:
+        keep = ctx.enter_context(tc.tile_pool(name="keep", bufs=1))
+        psum = ctx.enter_context(tc.psum_pool(name="psum", bufs=1))
+        ctx.enter_context(tc.manual_schedule())
+
+        xbytes, xscale, wraw, wgrp, wq, wsc = {}, {}, {}, {}, {}, {}
+        xwide, xsum, xturn, xgrp, xq, xsc = {}, {}, {}, {}, {}, {}
+        acc, logit, sig, prob, pbf, pturn, pgrp, pcodes = {}, {}, {}, {}, {}, {}, {}, {}
+        count = {"acc": 0, "turn": 0}
+
+        def bank(kind, banks, dtype=F32):
+            index = count[kind] % banks
+            count[kind] = count[kind] + 1
+            cols = GROUP if dtype == F32 else HALF
+            return psum.tile([P, cols], dtype, name="%s%d" % (kind, index))
+
+        def load_x(first, last):
+            t = keep.tile([P, last - first, K], U8, name="xbytes%d" % first)
+            nc.sync.dma_start(out=t[:], in_=X_bytes[first * P : last * P, :].rearrange("(i p) k -> p i k", p=P))
+            for i in range(first, last):
+                xbytes[i] = t[:, i - first, :]
+
+        def load_xscale(first, last):
+            t = keep.tile([P, last - first, 16], F32, name="xscale%d" % first)
+            nc.sync.dma_start(
+                out=t[:, :, 0:BLOCKS], in_=X_scale[first * P : last * P, :].rearrange("(i p) c -> p i c", p=P)
+            )
+            for i in range(first, last):
+                xscale[i] = t[:, i - first, :]
+
+        def load_w(c, first, last):
+            t = keep.tile([P, 4, (last - first) * GROUP], BF16, name="wraw%d_%d" % (c, first))
+            rows = W[c * GROUP : (c + 1) * GROUP, first * GROUP : last * GROUP]
+            nc.sync.dma_start(out=t[:], in_=rows.rearrange("(p j) n -> p j n", j=4))
+            for g in range(first, last):
+                wraw[c, g] = t[:, :, (g - first) * GROUP : (g - first + 1) * GROUP]
+
+        def load_row(row, parts, name):
+            t = keep.tile([P, row.shape[1] // P], BF16, name=name)
+            nc.sync.dma_start(
+                out=t[:].rearrange("p (h c) -> p h c", h=parts),
+                in_=row.rearrange("o (h p c) -> p (o h) c", h=parts, p=P),
+            )
+            return t[:].bitcast(F32)
+
+        def stage(slot):
+            return keep.tile([P, 4 * GROUP], BF16, name="stage%s" % slot, align_bytes=64)
+
+        def interleave_w(c, g, slot, engine):
+            t = stage(slot)
+            dst = t[:].rearrange("p (n i j) -> p n j i", i=4, j=4)
+            src = wraw[c, g].rearrange("p j (n i) -> p n j i", i=4)
+            if engine == "vector":
+                nc.vector.tensor_copy(out=dst, in_=src)
+            elif engine == "gpsimd":
+                dst = t[:].rearrange("p (n j) -> p n j", j=4)
+                src = wraw[c, g].rearrange("p j n -> p n j")
+                nc.gpsimd.tensor_scalar(out=dst, in0=src, scalar1=1.0, scalar2=0.0, op0=ALU.mult, op1=ALU.add)
+            else:
+                nc.scalar.copy(out=dst, in_=src)
+            wgrp[c, g] = t
+
+        def quantize_w(c, g):
+            wq[c, g] = keep.tile([P, GROUP], U32, name="wq%d_%d" % (c, g), align_bytes=64)
+            wsc[c, g] = keep.tile([P, GROUP], U8, name="wsc%d_%d" % (c, g), align_bytes=64)
+            nc.vector.quantize_mx(out=wq[c, g][:].bitcast(FP8X4), scales=wsc[c, g][:], in_=wgrp[c, g][:])
+
+        def widen_x(i, engine, first=0, last=BLOCKS):
+            if first == 0:
+                xwide[i] = keep.tile([P, K], F32, name="xwide", bufs=2)
+            for b in range(first, last):
+                cols = slice(b * BLOCK, (b + 1) * BLOCK)
+                src = xbytes[i][:, cols].bitcast(FP8)
+                if engine == "vector":
+                    nc.vector.tensor_scalar(
+                        out=xwide[i][:, cols], in0=src, scalar1=xscale[i][:, b : b + 1], scalar2=None, op0=ALU.mult
+                    )
+                else:
+                    nc.scalar.activation(out=xwide[i][:, cols], in_=src, func=ACT.Copy, scale=xscale[i][:, b : b + 1])
+
+        def add_mean(i, slot, engine):
+            xsum[i] = stage(slot)
+            engine.tensor_tensor(out=xsum[i][:, 0:K], in0=xwide[i][:], in1=mean_all[:], op=ALU.add)
+
+        def turn_x(i):
+            words = xsum[i][:, 0:K].bitcast(F32)
+            xturn[i] = [bank("turn", TURN_BANKS), bank("turn", TURN_BANKS)]
+            for c in range(PASSES):
+                for u in range(2):
+                    slot = (2 * c + u) % 4
+                    nc.tensor.transpose(
+                        xturn[i][c // 2][:, slot * P : (slot + 1) * P],
+                        words[:, 256 * c + u : 256 * (c + 1) : 2],
+                        ident[:],
+                    )
+
+        def group_x(i, slot):
+            xgrp[i] = stage(slot)
+            words = xgrp[i][:, 0:K].bitcast(F32)
+            nc.scalar.copy(
+                out=words[:, 0:512].rearrange("p (c r u) -> p c r u", c=2, u=2),
+                in_=xturn[i][0][:].rearrange("p (c u r) -> p c r u", c=2, u=2),
+            )
+            nc.scalar.copy(
+                out=words[:, 512:768].rearrange("p (r u) -> p r u", u=2),
+                in_=xturn[i][1][:, 0:256].rearrange("p (u r) -> p r u", u=2),
+            )
+
+        def quantize_x(i, part):
+            if i not in xq:
+                xq[i] = keep.tile([P, PASSES * P], U32, name="xq%d" % i, align_bytes=64)
+                xsc[i] = keep.tile([P, PASSES * P], U8, name="xsc%d" % i, align_bytes=64)
+            lo, hi = ((0, 256), (256, 384))[part]
+            nc.vector.quantize_mx(
+                out=xq[i][:, lo:hi].bitcast(FP8X4), scales=xsc[i][:, lo:hi], in_=xgrp[i][:, 4 * lo : 4 * hi]
+            )
+
+        def multiply(u, gl):
+            i, h = UNITS[u]
+            g = 2 * h + gl
+            acc[u, gl] = bank("acc", ACC_BANKS)
+            for c in range(PASSES):
+                cols = slice(c * P, (c + 1) * P)
+                nc.tensor.matmul_mx(
+                    out=acc[u, gl][:],
+                    lhsT=xq[i][:, cols].bitcast(FP8X4),
+                    lhsT_scale=xsc[i][:, cols],
+                    rhs=wq[c, g][:].bitcast(FP8X4),
+                    rhs_scale=wsc[c, g][:],
+                    start=(c == 0),
+                    stop=(c == PASSES - 1),
+                )
+
+        def add_item_bias(u, gl):
+            i, h = UNITS[u]
+            g = 2 * h + gl
+            if gl == 0:
+                logit[u] = keep.tile([P, HALF], F32, name="logit", bufs=2)
+            nc.vector.tensor_tensor(
+                out=logit[u][:, gl * GROUP : (gl + 1) * GROUP],
+                in0=acc[u, gl][:],
+                in1=item_all[:, g * GROUP : (g + 1) * GROUP],
+                op=ALU.add,
+            )
+
+        def sigmoid(u, lo=0, hi=HALF):
+            i, h = UNITS[u]
+            if lo == 0:
+                sig[u] = keep.tile([P, HALF], F32, name="sig", bufs=3)
+            nc.scalar.activation(out=sig[u][:, lo:hi], in_=logit[u][:, lo:hi], func=ACT.Sigmoid, bias=user_col[:, i : i + 1])
+
+        def weigh(u, lo=0, hi=HALF):
+            i, h = UNITS[u]
+            if lo == 0:
+                prob[u] = keep.tile([P, HALF], F32, name="prob", bufs=4)
+            nc.vector.tensor_tensor(out=prob[u][:, lo:hi], in0=sig[u][:, lo:hi], in1=exam_all[h][:, lo:hi], op=ALU.mult)
+            nc.sync.dma_start(
+                out=out_0[i * P : (i + 1) * P, h * HALF + lo : h * HALF + hi], in_=prob[u][:, lo:hi]
+            )
+
+        def round_y(u, engine, gls=(0, 1)):
+            if gls[0] == 0:
+                pbf[u] = keep.tile([P, HALF], BF16, name="pbf", bufs=3)
+            cols = slice(gls[0] * GROUP, (gls[-1] + 1) * GROUP)
+            dst = pbf[u][:, cols].rearrange("p (g u q e) -> p g u q e", u=2, q=P, e=2)
+            src = prob[u][:, cols].rearrange("p (g q u e) -> p g u q e", u=2, q=P, e=2)
+            if len(gls) == 1:
+                dst, src = dst[:, 0], src[:, 0]
+            if engine == "vector":
+                nc.vector.tensor_copy(out=dst, in_=src)
+            else:
+                nc.scalar.copy(out=dst, in_=src)
+
+        def turn_y(u, gls=(0, 1)):
+            words = pbf[u][:].bitcast(F32)
+            pturn[u, gls[0]] = bank("turn", TURN_BANKS)
+            for slot in range(2 * gls[0], 2 * gls[-1] + 2):
+                nc.tensor.transpose(
+                    pturn[u, gls[0]][:, slot * P : (slot + 1) * P], words[:, slot * P : (slot + 1) * P], ident[:]
+                )
+
+        def group_y(u, slot, gls=(0, 1)):
+            if gls[0] == 0:
+                pgrp[u] = stage(slot)
+            cols = slice(gls[0] * 256, (gls[-1] + 1) * 256)
+            nc.scalar.copy(
+                out=pgrp[u][:, 0:HALF].bitcast(F32)[:, cols].rearrange("p (g r u) -> p g r u", r=P, u=2),
+                in_=pturn[u, gls[0]][:, cols].rearrange("p (g u r) -> p g r u", r=P, u=2),
+            )
+
+        def quantize_y(u, gl):
+            i, h = UNITS[u]
+            g = 2 * h + gl
+            if gl == 0:
+                pcodes[u] = keep.tile([P, 2 * P], U32, name="pcodes", bufs=3, align_bytes=64)
+            nc.vector.quantize_mx(
+                out=pcodes[u][:, gl * P : (gl + 1) * P].bitcast(FP8X4),
+                scales=pscales[4 * g : P, i * P : (i + 1) * P],
+                in_=pgrp[u][:, gl * GROUP : (gl + 1) * GROUP],
+            )
+            if gl == 1:
+                nc.sync.dma_start(
+                    out=words_out[:, 2 * h : 2 * h + 2, i * P : (i + 1) * P],
+                    in_=pcodes[u][:].bitcast(I32).rearrange("p (g m) -> p g m", g=2),
+                )
+
+        def spread(words, first, out, step):
+            for w in range(out.shape[1] // P):
+                dst = out[:, w * P : (w + 1) * P] if step == 1 else out[:, w : step * P : step]
+                nc.tensor.transpose(dst, words[:, first + w : first + w + 1].to_broadcast([P, P]), ident[:])
+
+        ident = keep.tile([P, P], F32, name="ident")
+        ident_bf = keep.tile([P, P], BF16, name="ident_bf")
+        user_rows = keep.tile([P, P], BF16, name="user_rows")
+        user_col = keep.tile([P, TILES], F32, name="user_col")
+        mean_all = keep.tile([P, K], BF16, name="mean_all")
+        item_all = keep.tile([P, N], BF16, name="item_all")
+        pscales = keep.tile([P, T], U8, name="pscales", align_bytes=64)
+        warm = keep.tile([P, 2], F32, name="warm")
+
+        def spread_mean():
+            banks = [bank("turn", TURN_BANKS), bank("turn", TURN_BANKS)]
+            spread(mean_words, 0, banks[0][:], 1)
+            spread(mean_words, 4, banks[1][:, 0:256], 1)
+            return banks
+
+        def copy_mean(banks):
+            words = mean_all[:].bitcast(F32)
+            nc.scalar.copy(
+                out=words[:, 0:512].rearrange("p (c j w) -> p c j w", c=2, w=2),
+                in_=banks[0][:].rearrange("p (c w j) -> p c j w", c=2, w=2),
+            )
+            nc.scalar.copy(
+                out=words[:, 512:768].rearrange("p (j w) -> p j w", w=2),
+                in_=banks[1][:, 0:256].rearrange("p (w j) -> p j w", w=2),
+            )
+
+        def spread_item(h):
+            b = bank("turn", TURN_BANKS)
+            spread(item_words, 4 * h, b[:], 1)
+            return b
+
+        def copy_item(h, b, copy):
+            copy(
+                out=item_all[:].bitcast(F32)[:, h * GROUP : (h + 1) * GROUP].rearrange("p (j w) -> p j w", w=4),
+                in_=b[:].rearrange("p (w j) -> p j w", w=4),
+            )
+
+        def spread_exam(h):
+            b = psum.tile([P, GROUP], F32, name="exam%d" % h)
+            spread(exam_words, 4 * h, b[:], 4)
+            return b[:].bitcast(BF16)
+
+        def turn_user():
+            b = bank("turn", TURN_BANKS, BF16)
+            nc.tensor.transpose(b[:, 0:P], user_rows[:], ident_bf[:])
+            nc.scalar.copy(out=user_col[:], in_=b[:, 0:TILES])
+
+        def store_scales():
+            for quad in range(4):
+                nc.sync.dma_start(
+                    out=scales_out[:, 4 * quad : 4 * quad + 4, :],
+                    in_=pscales[32 * quad : 32 * quad + 16, :].bitcast(I32),
+                )
+
+
+        load_x(0, 1)
+        load_xscale(0, 2)
+        load_w(0, 0, 1)
+        mean_words = load_row(X_mean, PASSES, "mean_row")
+        load_w(0, 1, 2)
+        load_w(1, 0, 2)
+        load_x(1, 2)
+        load_w(2, 0, 2)
+        item_words = load_row(item_bias, 2, "item_row")
+        exam_words = load_row(exam, 2, "exam_row")
+        make_identity(nc, ident[:])
+        nc.gpsimd.memset(user_rows[:], 0.0)
+        make_identity(nc, ident_bf[:])
+        nc.sync.dma_start(out=user_rows[0:TILES, :], in_=user_bias.rearrange("(i p) o -> i (p o)", p=P))
+        load_xscale(2, TILES)
+        load_x(2, 4)
+        load_w(0, 2, 4)
+        load_w(1, 2, 4)
+        load_w(2, 2, 4)
+        load_x(4, TILES)
+        nc.vector.memset(warm[:, 0:1], 0.0)
+        nc.scalar.activation(out=warm[:, 1:2], in_=warm[:, 0:1], func=ACT.Sigmoid)
+
+        widen_x(0, "scalar")
+        copy_mean(spread_mean())
+        interleave_w(0, 0, "a", "vector")
+        interleave_w(0, 1, "b", "vector")
+        quantize_w(0, 0)
+        add_mean(0, "c", nc.vector)
+        interleave_w(1, 1, "d", "scalar")
+        turn_x(0)
+        quantize_w(0, 1)
+        interleave_w(1, 0, "a", "vector")
+        group_x(0, "x0")
+        widen_x(1, "scalar")
+        quantize_w(1, 1)
+        quantize_w(1, 0)
+        interleave_w(2, 0, "b", "vector")
+        quantize_x(0, 0)
+        quantize_x(0, 1)
+        interleave_w(2, 1, "e", "scalar")
+        item0 = spread_item(0)
+        add_mean(1, "c", nc.vector)
+        quantize_w(2, 0)
+        multiply(0, 0)
+        turn_x(1)
+        copy_item(0, item0, nc.vector.tensor_copy)
+        group_x(1, "x1")
+        turn_user()
+        widen_x(2, "scalar")
+        interleave_w(0, 2, "a", "vector")
+        quantize_w(2, 1)
+        multiply(0, 1)
+        exam_all = [spread_exam(0)]
+        item1 = spread_item(1)
+        quantize_x(1, 0)
+        quantize_x(1, 1)
+        quantize_w(0, 2)
+        add_mean(2, "a", nc.gpsimd)
+        interleave_w(0, 3, "b", "scalar")
+        add_item_bias(0, 0)
+        multiply(1, 0)
+        add_item_bias(0, 1)
+        multiply(1, 1)
+        exam_all.append(spread_exam(1))
+        copy_item(1, item1, nc.vector.tensor_copy)
+        sigmoid(0)
+        add_item_bias(1, 0)
+        add_item_bias(1, 1)
+        weigh(0)
+        widen_x(3, "scalar")
+        turn_x(2)
+        interleave_w(1, 2, "c", "vector")
+        quantize_w(0, 3)
+        interleave_w(2, 2, "d", "vector")
+        quantize_w(1, 2)
+        sigmoid(1)
+        group_x(2, "x0")
+        add_mean(3, "a", nc.vector)
+        interleave_w(1, 3, "b", "scalar")
+        quantize_w(2, 2)
+        multiply(2, 0)
+        turn_x(3)
+        interleave_w(2, 3, "e", "vector")
+        round_y(0, "vector")
+        turn_y(0)
+        widen_x(4, "scalar")
+        group_x(3, "x1")
+        quantize_x(2, 0)
+        quantize_w(1, 3)
+        quantize_x(2, 1)
+        quantize_w(2, 3)
+        multiply(2, 1)
+        last_slot = "e"
+        for cyc in range(1, TILES):
+            a = 2 * cyc
+            j = cyc + 3
+            slot = ("e", "d")[cyc % 2]
+            if j < TILES:
+                add_mean(j, last_slot, nc.gpsimd)
+            if cyc > 1:
+                group_y(a - 4, "b")
+                group_y(a - 3, slot)
+            add_item_bias(a, 0)
+            multiply(a + 1, 0)
+            if cyc > 1:
+                weigh(a - 2)
+            if j + 1 < TILES:
+                widen_x(j + 1, "scalar", 0, 6)
+            add_item_bias(a, 1)
+            if j + 1 >= TILES:
+                round_y(a - 2, "scalar")
+            sigmoid(a)
+            multiply(a + 1, 1)
+            add_item_bias(a + 1, 0)
+            if cyc < TILES - 1:
+                multiply(a + 2, 0)
+            weigh(a - 1)
+            if j + 1 < TILES:
+                widen_x(j + 1, "scalar", 6, 12)
+            add_item_bias(a + 1, 1)
+            if cyc == TILES - 1:
+                break
+            sigmoid(a + 1)
+            if j < TILES:
+                turn_x(j)
+                group_x(j, "x%d" % (j % 2))
+            multiply(a + 2, 1)
+            if cyc == 1:
+                round_y(1, "vector")
+                turn_y(1)
+                quantize_x(3, 0)
+                quantize_x(3, 1)
+                last_slot = "x1"
+                continue
+            if j + 1 < TILES:
+                round_y(a - 2, "vector")
+            turn_y(a - 2)
+            quantize_y(a - 4, 0)
+            round_y(a - 1, "vector" if j < TILES else "scalar")
+            turn_y(a - 1)
+            quantize_y(a - 4, 1)
+            if j - 1 < TILES:
+                quantize_x(j - 1, 0)
+            quantize_y(a - 3, 0)
+            if j - 1 < TILES:
+                quantize_x(j - 1, 1)
+            quantize_y(a - 3, 1)
+            last_slot = slot
+        sigmoid(15, 0, GROUP)
+        turn_y(12)
+        weigh(14)
+        sigmoid(15, GROUP, HALF)
+        quantize_y(10, 0)
+        round_y(13, "vector")
+        turn_y(13)
+        quantize_y(10, 1)
+        group_y(12, "a")
+        weigh(15, 0, GROUP)
+        quantize_y(11, 0)
+        round_y(14, "vector")
+        turn_y(14)
+        group_y(13, "c")
+        quantize_y(11, 1)
+        weigh(15, GROUP, HALF)
+        quantize_y(12, 0)
+        round_y(15, "vector", (0,))
+        turn_y(15, (0,))
+        group_y(14, "b")
+        quantize_y(12, 1)
+        round_y(15, "vector", (1,))
+        turn_y(15, (1,))
+        group_y(15, "d", (0,))
+        group_y(15, "d", (1,))
+        quantize_y(13, 0)
+        quantize_y(14, 0)
+        quantize_y(13, 1)
+        quantize_y(14, 1)
+        quantize_y(15, 0)
+        quantize_y(15, 1)
+        store_scales()

@@ -23,8 +23,8 @@ HALF = 1024
 TILES = 8
 BLOCK = 128
 BLOCKS = 12
-ACC_BANKS = 2
-TURN_BANKS = 4
+ACC_BANKS = 3
+TURN_BANKS = 3
 UNITS = [(0, 0), (1, 0), (0, 1), (1, 1)] + [(i, h) for i in range(2, TILES) for h in range(2)]
 
 
@@ -44,6 +44,7 @@ def tile_centred_click_probability_b15_kernel(
         xwide, xsum, xturn, xgrp, xq, xsc = {}, {}, {}, {}, {}, {}
         acc, logit, sig, prob, pbf, pturn, pgrp, pcodes = {}, {}, {}, {}, {}, {}, {}, {}
         count = {"acc": 0, "turn": 0}
+        exam_all = {}
 
         def bank(kind, banks, dtype=F32):
             index = count[kind] % banks
@@ -57,9 +58,9 @@ def tile_centred_click_probability_b15_kernel(
             for i in range(first, last):
                 xbytes[i] = t[:, i - first, :]
 
-        def load_xscale(first, last):
+        def load_xscale(first, last, queue):
             t = keep.tile([P, last - first, 16], F32, name="xscale%d" % first)
-            nc.sync.dma_start(
+            queue.dma_start(
                 out=t[:, :, 0:BLOCKS], in_=X_scale[first * P : last * P, :].rearrange("(i p) c -> p i c", p=P)
             )
             for i in range(first, last):
@@ -72,9 +73,9 @@ def tile_centred_click_probability_b15_kernel(
             for g in range(first, last):
                 wraw[c, g] = t[:, :, (g - first) * GROUP : (g - first + 1) * GROUP]
 
-        def load_row(row, parts, name):
+        def load_row(row, parts, name, queue):
             t = keep.tile([P, row.shape[1] // P], BF16, name=name)
-            nc.sync.dma_start(
+            queue.dma_start(
                 out=t[:].rearrange("p (h c) -> p h c", h=parts),
                 in_=row.rearrange("o (h p c) -> p (o h) c", h=parts, p=P),
             )
@@ -104,7 +105,7 @@ def tile_centred_click_probability_b15_kernel(
 
         def widen_x(i, engine, first=0, last=BLOCKS):
             if first == 0:
-                xwide[i] = keep.tile([P, K], F32, name="xwide", bufs=2)
+                xwide[i] = keep.tile([P, K], F32, name="xwide", bufs=3)
             for b in range(first, last):
                 cols = slice(b * BLOCK, (b + 1) * BLOCK)
                 src = xbytes[i][:, cols].bitcast(FP8)
@@ -117,7 +118,8 @@ def tile_centred_click_probability_b15_kernel(
 
         def add_mean(i, slot, engine):
             xsum[i] = stage(slot)
-            engine.tensor_tensor(out=xsum[i][:, 0:K], in0=xwide[i][:], in1=mean_all[:], op=ALU.add)
+            add = nc.vector.tensor_tensor if engine == "vector" else nc.gpsimd.tensor_tensor
+            add(out=xsum[i][:, 0:K], in0=xwide[i][:], in1=mean_all[:], op=ALU.add)
 
         def turn_x(i):
             words = xsum[i][:, 0:K].bitcast(F32)
@@ -131,14 +133,14 @@ def tile_centred_click_probability_b15_kernel(
                         ident[:],
                     )
 
-        def group_x(i, slot):
+        def group_x(i, slot, copy):
             xgrp[i] = stage(slot)
             words = xgrp[i][:, 0:K].bitcast(F32)
-            nc.scalar.copy(
+            copy(
                 out=words[:, 0:512].rearrange("p (c r u) -> p c r u", c=2, u=2),
                 in_=xturn[i][0][:].rearrange("p (c u r) -> p c r u", c=2, u=2),
             )
-            nc.scalar.copy(
+            copy(
                 out=words[:, 512:768].rearrange("p (r u) -> p r u", u=2),
                 in_=xturn[i][1][:, 0:256].rearrange("p (u r) -> p r u", u=2),
             )
@@ -195,32 +197,36 @@ def tile_centred_click_probability_b15_kernel(
                 out=out_0[i * P : (i + 1) * P, h * HALF + lo : h * HALF + hi], in_=prob[u][:, lo:hi]
             )
 
-        def round_y(u, engine, gls=(0, 1)):
+        def round_y(u, engine, slot, gls=(0, 1)):
             if gls[0] == 0:
-                pbf[u] = keep.tile([P, HALF], BF16, name="pbf", bufs=3)
+                pbf[u] = stage(slot)
             cols = slice(gls[0] * GROUP, (gls[-1] + 1) * GROUP)
-            dst = pbf[u][:, cols].rearrange("p (g u q e) -> p g u q e", u=2, q=P, e=2)
-            src = prob[u][:, cols].rearrange("p (g q u e) -> p g u q e", u=2, q=P, e=2)
-            if len(gls) == 1:
-                dst, src = dst[:, 0], src[:, 0]
             if engine == "vector":
-                nc.vector.tensor_copy(out=dst, in_=src)
+                nc.vector.tensor_copy(out=pbf[u][:, cols], in_=prob[u][:, cols])
+            elif engine == "gpsimd":
+                nc.gpsimd.tensor_scalar(
+                    out=pbf[u][:, cols], in0=prob[u][:, cols], scalar1=1.0, scalar2=0.0, op0=ALU.mult, op1=ALU.add
+                )
             else:
-                nc.scalar.copy(out=dst, in_=src)
+                nc.scalar.copy(out=pbf[u][:, cols], in_=prob[u][:, cols])
 
         def turn_y(u, gls=(0, 1)):
-            words = pbf[u][:].bitcast(F32)
+            words = pbf[u][:, 0:HALF].bitcast(F32)
             pturn[u, gls[0]] = bank("turn", TURN_BANKS)
-            for slot in range(2 * gls[0], 2 * gls[-1] + 2):
-                nc.tensor.transpose(
-                    pturn[u, gls[0]][:, slot * P : (slot + 1) * P], words[:, slot * P : (slot + 1) * P], ident[:]
-                )
+            for gl in gls:
+                for half in range(2):
+                    slot = 2 * gl + half
+                    nc.tensor.transpose(
+                        pturn[u, gls[0]][:, slot * P : (slot + 1) * P],
+                        words[:, 256 * gl + half : 256 * (gl + 1) : 2],
+                        ident[:],
+                    )
 
-        def group_y(u, slot, gls=(0, 1)):
+        def group_y(u, slot, copy, gls=(0, 1)):
             if gls[0] == 0:
                 pgrp[u] = stage(slot)
             cols = slice(gls[0] * 256, (gls[-1] + 1) * 256)
-            nc.scalar.copy(
+            copy(
                 out=pgrp[u][:, 0:HALF].bitcast(F32)[:, cols].rearrange("p (g r u) -> p g r u", r=P, u=2),
                 in_=pturn[u, gls[0]][:, cols].rearrange("p (g u r) -> p g r u", r=P, u=2),
             )
@@ -293,6 +299,9 @@ def tile_centred_click_probability_b15_kernel(
             nc.tensor.transpose(b[:, 0:P], user_rows[:], ident_bf[:])
             nc.scalar.copy(out=user_col[:], in_=b[:, 0:TILES])
 
+        def load_user():
+            nc.sync.dma_start(out=user_rows[0:TILES, :], in_=user_bias.rearrange("(i p) o -> i (p o)", p=P))
+
         def store_scales():
             for quad in range(4):
                 nc.sync.dma_start(
@@ -300,185 +309,298 @@ def tile_centred_click_probability_b15_kernel(
                     in_=pscales[32 * quad : 32 * quad + 16, :].bitcast(I32),
                 )
 
-
-        load_x(0, 1)
-        load_xscale(0, 2)
-        load_w(0, 0, 1)
-        mean_words = load_row(X_mean, PASSES, "mean_row")
-        load_w(0, 1, 2)
-        load_w(1, 0, 2)
-        load_x(1, 2)
-        load_w(2, 0, 2)
-        item_words = load_row(item_bias, 2, "item_row")
-        exam_words = load_row(exam, 2, "exam_row")
-        make_identity(nc, ident[:])
-        nc.gpsimd.memset(user_rows[:], 0.0)
         make_identity(nc, ident_bf[:])
-        nc.sync.dma_start(out=user_rows[0:TILES, :], in_=user_bias.rearrange("(i p) o -> i (p o)", p=P))
-        load_xscale(2, TILES)
-        load_x(2, 4)
-        load_w(0, 2, 4)
-        load_w(1, 2, 4)
-        load_w(2, 2, 4)
-        load_x(4, TILES)
+        mean_words = load_row(X_mean, PASSES, "mean_row", nc.scalar)
+        nc.gpsimd.memset(user_rows[:], 0.0)
+        load_xscale(0, 2, nc.scalar)
+        load_x(0, 1)
+        load_x(1, 2)
         nc.vector.memset(warm[:, 0:1], 0.0)
         nc.scalar.activation(out=warm[:, 1:2], in_=warm[:, 0:1], func=ACT.Sigmoid)
-
-        widen_x(0, "scalar")
+        widen_x(0, "scalar", 0, 6)
+        load_w(0, 0, 1)
+        load_w(0, 1, 2)
+        widen_x(0, "vector", 6, 12)
+        make_identity(nc, ident[:])
+        load_user()
+        item_words = load_row(item_bias, 2, "item_row", nc.sync)
         copy_mean(spread_mean())
-        interleave_w(0, 0, "a", "vector")
-        interleave_w(0, 1, "b", "vector")
-        quantize_w(0, 0)
-        add_mean(0, "c", nc.vector)
-        interleave_w(1, 1, "d", "scalar")
+        widen_x(1, "vector", 0, 6)
+        interleave_w(0, 0, "c", "vector")
+        load_w(1, 0, 2)
+        add_mean(0, "g", "vector")
+        widen_x(1, "scalar", 6, 12)
+        load_w(2, 0, 2)
         turn_x(0)
-        quantize_w(0, 1)
-        interleave_w(1, 0, "a", "vector")
-        group_x(0, "x0")
-        widen_x(1, "scalar")
-        quantize_w(1, 1)
-        quantize_w(1, 0)
-        interleave_w(2, 0, "b", "vector")
-        quantize_x(0, 0)
-        quantize_x(0, 1)
-        interleave_w(2, 1, "e", "scalar")
-        item0 = spread_item(0)
-        add_mean(1, "c", nc.vector)
-        quantize_w(2, 0)
-        multiply(0, 0)
+        interleave_w(0, 1, "f", "scalar")
+        group_x(0, "d", nc.scalar.copy)
+        quantize_w(0, 0)
+        exam_words = load_row(exam, 2, "exam_row", nc.sync)
+        load_xscale(2, TILES, nc.sync)
+        load_x(2, 4)
+        add_mean(1, "a", "vector")
+        interleave_w(1, 1, "i", "scalar")
         turn_x(1)
-        copy_item(0, item0, nc.vector.tensor_copy)
-        group_x(1, "x1")
+        load_w(0, 2, 4)
+        group_x(1, "c", nc.scalar.copy)
+        quantize_w(0, 1)
+        item0 = spread_item(0)
+        quantize_x(0, 0)
+        interleave_w(2, 1, "h", "scalar")
         turn_user()
-        widen_x(2, "scalar")
-        interleave_w(0, 2, "a", "vector")
-        quantize_w(2, 1)
-        multiply(0, 1)
-        exam_all = [spread_exam(0)]
-        item1 = spread_item(1)
-        quantize_x(1, 0)
+        load_x(4, TILES)
+        load_w(1, 2, 4)
+        load_w(2, 2, 4)
+        interleave_w(1, 0, "e", "vector")
+        copy_item(0, item0, nc.vector.tensor_copy)
+        quantize_w(1, 0)
+        quantize_w(1, 1)
+        interleave_w(2, 0, "e", "vector")
+        widen_x(3, "scalar", 0, 6)
+        widen_x(2, "scalar", 0, 6)
         quantize_x(1, 1)
+        exam_all[0] = spread_exam(0)
+        widen_x(2, "scalar", 6, 12)
+        quantize_w(2, 0)
+        quantize_w(2, 1)
+        quantize_x(0, 1)
+        interleave_w(0, 2, "a", "vector")
+        exam_all[1] = spread_exam(1)
+        item1 = spread_item(1)
+        multiply(0, 0)
+        quantize_x(1, 0)
+        widen_x(3, "vector", 6, 12)
+        multiply(0, 1)
         quantize_w(0, 2)
-        add_mean(2, "a", nc.gpsimd)
-        interleave_w(0, 3, "b", "scalar")
         add_item_bias(0, 0)
+        interleave_w(0, 3, "d", "scalar")
         multiply(1, 0)
         add_item_bias(0, 1)
-        multiply(1, 1)
-        exam_all.append(spread_exam(1))
-        copy_item(1, item1, nc.vector.tensor_copy)
         sigmoid(0)
+        multiply(1, 1)
         add_item_bias(1, 0)
+        copy_item(1, item1, nc.vector.tensor_copy)
         add_item_bias(1, 1)
         weigh(0)
-        widen_x(3, "scalar")
-        turn_x(2)
-        interleave_w(1, 2, "c", "vector")
-        quantize_w(0, 3)
-        interleave_w(2, 2, "d", "vector")
+        interleave_w(1, 2, "f", "vector")
+        interleave_w(2, 2, "e", "vector")
+        add_mean(2, "a", "gpsimd")
         quantize_w(1, 2)
-        sigmoid(1)
-        group_x(2, "x0")
-        add_mean(3, "a", nc.vector)
-        interleave_w(1, 3, "b", "scalar")
+        round_y(0, "vector", "h")
+        interleave_w(1, 3, "c", "scalar")
         quantize_w(2, 2)
-        multiply(2, 0)
-        turn_x(3)
-        interleave_w(2, 3, "e", "vector")
-        round_y(0, "vector")
-        turn_y(0)
-        widen_x(4, "scalar")
-        group_x(3, "x1")
-        quantize_x(2, 0)
+        turn_x(2)
         quantize_w(1, 3)
-        quantize_x(2, 1)
+        interleave_w(2, 3, "b", "scalar")
+        multiply(2, 0)
+        quantize_w(0, 3)
         quantize_w(2, 3)
+        widen_x(4, "scalar", 0, 6)
+        group_x(2, "f", nc.vector.tensor_copy)
         multiply(2, 1)
-        last_slot = "e"
-        for cyc in range(1, TILES):
-            a = 2 * cyc
-            j = cyc + 3
-            slot = ("e", "d")[cyc % 2]
-            if j < TILES:
-                add_mean(j, last_slot, nc.gpsimd)
-            if cyc > 1:
-                group_y(a - 4, "b")
-                group_y(a - 3, slot)
-            add_item_bias(a, 0)
-            multiply(a + 1, 0)
-            if cyc > 1:
-                weigh(a - 2)
-            if j + 1 < TILES:
-                widen_x(j + 1, "scalar", 0, 6)
-            add_item_bias(a, 1)
-            if j + 1 >= TILES:
-                round_y(a - 2, "scalar")
-            sigmoid(a)
-            multiply(a + 1, 1)
-            add_item_bias(a + 1, 0)
-            if cyc < TILES - 1:
-                multiply(a + 2, 0)
-            weigh(a - 1)
-            if j + 1 < TILES:
-                widen_x(j + 1, "scalar", 6, 12)
-            add_item_bias(a + 1, 1)
-            if cyc == TILES - 1:
-                break
-            sigmoid(a + 1)
-            if j < TILES:
-                turn_x(j)
-                group_x(j, "x%d" % (j % 2))
-            multiply(a + 2, 1)
-            if cyc == 1:
-                round_y(1, "vector")
-                turn_y(1)
-                quantize_x(3, 0)
-                quantize_x(3, 1)
-                last_slot = "x1"
-                continue
-            if j + 1 < TILES:
-                round_y(a - 2, "vector")
-            turn_y(a - 2)
-            quantize_y(a - 4, 0)
-            round_y(a - 1, "vector" if j < TILES else "scalar")
-            turn_y(a - 1)
-            quantize_y(a - 4, 1)
-            if j - 1 < TILES:
-                quantize_x(j - 1, 0)
-            quantize_y(a - 3, 0)
-            if j - 1 < TILES:
-                quantize_x(j - 1, 1)
-            quantize_y(a - 3, 1)
-            last_slot = slot
-        sigmoid(15, 0, GROUP)
-        turn_y(12)
-        weigh(14)
-        sigmoid(15, GROUP, HALF)
+        multiply(3, 0)
+        sigmoid(1)
+        add_item_bias(2, 0)
+        add_mean(3, "b", "gpsimd")
+        weigh(1)
+        add_item_bias(2, 1)
+        turn_y(0)
+        round_y(1, "scalar", "i")
+        multiply(3, 1)
+        add_item_bias(3, 0)
+        add_item_bias(3, 1)
+        quantize_x(2, 1)
+        sigmoid(2)
+        turn_x(3)
+        quantize_x(2, 0)
+        sigmoid(3)
+        multiply(4, 0)
+        group_y(0, "d", nc.vector.tensor_copy)
+        multiply(4, 1)
+        turn_y(1)
+        group_x(3, "h", nc.scalar.copy)
+        multiply(5, 0)
+        widen_x(4, "vector", 6, 12)
+        add_mean(4, "x0", "gpsimd")
+        widen_x(5, "scalar", 0, 6)
+        group_y(1, "e", nc.scalar.copy)
+        weigh(2)
+        add_item_bias(4, 0)
+        multiply(5, 1)
+        add_item_bias(4, 1)
+        sigmoid(4)
+        weigh(3)
+        round_y(2, "scalar", "g", (0,))
+        widen_x(5, "scalar", 6, 12)
+        add_item_bias(5, 0)
+        add_item_bias(5, 1)
+        turn_x(4)
+        sigmoid(5)
+        group_x(4, "x0", nc.scalar.copy)
+        quantize_y(0, 0)
+        quantize_x(3, 0)
+        quantize_x(3, 1)
+        multiply(6, 0)
+        multiply(6, 1)
+        multiply(7, 0)
+        quantize_y(0, 1)
+        round_y(2, "vector", "g", (1,))
+        turn_y(2)
+        quantize_y(1, 0)
+        round_y(3, "vector", "h")
+        turn_y(3)
+        quantize_y(1, 1)
+        add_mean(5, "e", "gpsimd")
+        widen_x(6, "scalar", 0, 6)
+        group_y(2, "b", nc.scalar.copy)
+        group_y(3, "d", nc.scalar.copy)
+        weigh(4)
+        add_item_bias(6, 0)
+        multiply(7, 1)
+        add_item_bias(6, 1)
+        sigmoid(6)
+        weigh(5)
+        round_y(4, "scalar", "g", (0,))
+        widen_x(6, "scalar", 6, 12)
+        add_item_bias(7, 0)
+        add_item_bias(7, 1)
+        turn_x(5)
+        sigmoid(7)
+        group_x(5, "x1", nc.scalar.copy)
+        quantize_y(2, 0)
+        quantize_x(4, 0)
+        quantize_x(4, 1)
+        multiply(8, 0)
+        multiply(8, 1)
+        multiply(9, 0)
+        quantize_y(2, 1)
+        round_y(4, "vector", "g", (1,))
+        turn_y(4)
+        quantize_y(3, 0)
+        round_y(5, "vector", "h")
+        turn_y(5)
+        quantize_y(3, 1)
+        add_mean(6, "d", "gpsimd")
+        widen_x(7, "scalar", 0, 6)
+        group_y(4, "b", nc.scalar.copy)
+        group_y(5, "e", nc.scalar.copy)
+        weigh(6)
+        add_item_bias(8, 0)
+        multiply(9, 1)
+        add_item_bias(8, 1)
+        sigmoid(8)
+        weigh(7)
+        round_y(6, "scalar", "g", (0,))
+        widen_x(7, "scalar", 6, 12)
+        add_item_bias(9, 0)
+        add_item_bias(9, 1)
+        turn_x(6)
+        sigmoid(9)
+        group_x(6, "x0", nc.scalar.copy)
+        quantize_y(4, 0)
+        quantize_x(5, 0)
+        quantize_x(5, 1)
+        multiply(10, 0)
+        multiply(10, 1)
+        multiply(11, 0)
+        quantize_y(4, 1)
+        round_y(6, "vector", "g", (1,))
+        turn_y(6)
+        quantize_y(5, 0)
+        round_y(7, "vector", "h")
+        turn_y(7)
+        quantize_y(5, 1)
+        add_mean(7, "e", "gpsimd")
+        group_y(6, "b", nc.scalar.copy)
+        group_y(7, "d", nc.scalar.copy)
+        weigh(8)
+        add_item_bias(10, 0)
+        multiply(11, 1)
+        add_item_bias(10, 1)
+        sigmoid(10)
+        weigh(9)
+        round_y(8, "scalar", "g")
+        add_item_bias(11, 0)
+        add_item_bias(11, 1)
+        turn_x(7)
+        sigmoid(11)
+        group_x(7, "x1", nc.scalar.copy)
+        quantize_y(6, 0)
+        quantize_x(6, 0)
+        quantize_x(6, 1)
+        multiply(12, 0)
+        multiply(12, 1)
+        multiply(13, 0)
+        quantize_y(6, 1)
+        turn_y(8)
+        quantize_y(7, 0)
+        round_y(9, "vector", "h")
+        turn_y(9)
+        quantize_y(7, 1)
+        weigh(10)
+        group_y(8, "a", nc.scalar.copy)
+        group_y(9, "i", nc.scalar.copy)
+        add_item_bias(12, 0)
+        multiply(13, 1)
+        weigh(11)
+        round_y(10, "gpsimd", "d")
+        add_item_bias(12, 1)
+        add_item_bias(13, 0)
+        quantize_y(8, 0)
+        quantize_x(7, 0)
+        quantize_x(7, 1)
+        sigmoid(12)
+        turn_y(10)
+        multiply(14, 0)
+        quantize_y(9, 0)
+        group_y(10, "h", nc.scalar.copy)
+        add_item_bias(13, 1)
+        quantize_y(8, 1)
+        multiply(14, 1)
+        weigh(12)
+        add_item_bias(14, 0)
+        sigmoid(13)
+        add_item_bias(14, 1)
+        quantize_y(9, 1)
+        multiply(15, 0)
         quantize_y(10, 0)
-        round_y(13, "vector")
-        turn_y(13)
+        round_y(11, "gpsimd", "a")
+        weigh(13)
+        round_y(12, "scalar", "d")
+        sigmoid(14)
         quantize_y(10, 1)
-        group_y(12, "a")
-        weigh(15, 0, GROUP)
+        add_item_bias(15, 0)
+        weigh(14)
+        turn_y(11)
+        group_y(11, "b", nc.scalar.copy)
+        turn_y(12)
+        group_y(12, "x0", nc.scalar.copy)
         quantize_y(11, 0)
-        round_y(14, "vector")
-        turn_y(14)
-        group_y(13, "c")
-        quantize_y(11, 1)
-        weigh(15, GROUP, HALF)
+        round_y(13, "scalar", "c")
+        sigmoid(15, 0, GROUP)
+        multiply(15, 1)
+        add_item_bias(15, 1)
+        sigmoid(15, GROUP, HALF)
         quantize_y(12, 0)
-        round_y(15, "vector", (0,))
-        turn_y(15, (0,))
-        group_y(14, "b")
+        quantize_y(11, 1)
+        round_y(14, "vector", "i")
         quantize_y(12, 1)
-        round_y(15, "vector", (1,))
-        turn_y(15, (1,))
-        group_y(15, "d", (0,))
-        group_y(15, "d", (1,))
+        turn_y(13)
+        weigh(15, 0, GROUP)
+        turn_y(14)
+        group_y(13, "a", nc.scalar.copy)
+        weigh(15, GROUP, HALF)
+        round_y(15, "vector", "d", (0,))
+        group_y(14, "b", nc.vector.tensor_copy)
+        round_y(15, "scalar", "b", (1,))
         quantize_y(13, 0)
         quantize_y(14, 0)
         quantize_y(13, 1)
+        turn_y(15, (0,))
+        turn_y(15, (1,))
+        group_y(15, "i", nc.scalar.copy, (0,))
         quantize_y(14, 1)
+        group_y(15, "a", nc.scalar.copy, (1,))
         quantize_y(15, 0)
         quantize_y(15, 1)
         store_scales()

@@ -44,7 +44,7 @@ def tile_centred_click_probability_b15_kernel(
         xwide, xsum, xturn, xgrp, xq, xsc = {}, {}, {}, {}, {}, {}
         acc, logit, sig, prob, pbf, pturn, pgrp, pcodes = {}, {}, {}, {}, {}, {}, {}, {}
         count = {"acc": 0, "turn": 0}
-        exam_all = {}
+        exam_all, mean_banks = {}, {}
 
         def bank(kind, banks, dtype=F32):
             index = count[kind] % banks
@@ -118,6 +118,15 @@ def tile_centred_click_probability_b15_kernel(
 
         def add_mean(i, slot, engine):
             xsum[i] = stage(slot)
+            if engine == "psum":
+                for lo, hi in ((0, HALF), (HALF, K)):
+                    nc.vector.tensor_tensor(
+                        out=xsum[i][:, lo:hi],
+                        in0=xwide[i][:, lo:hi],
+                        in1=mean_banks[lo // HALF][:].bitcast(BF16)[:, 0 : hi - lo],
+                        op=ALU.add,
+                    )
+                return
             add = nc.vector.tensor_tensor if engine == "vector" else nc.gpsimd.tensor_tensor
             add(out=xsum[i][:, 0:K], in0=xwide[i][:], in1=mean_all[:], op=ALU.add)
 
@@ -157,7 +166,8 @@ def tile_centred_click_probability_b15_kernel(
         def multiply(u, gl):
             i, h = UNITS[u]
             g = 2 * h + gl
-            acc[u, gl] = bank("acc", ACC_BANKS)
+            if (u, gl) not in acc:
+                acc[u, gl] = bank("acc", ACC_BANKS)
             for c in range(PASSES):
                 cols = slice(c * P, (c + 1) * P)
                 nc.tensor.matmul_mx(
@@ -168,6 +178,21 @@ def tile_centred_click_probability_b15_kernel(
                     rhs_scale=wsc[c, g][:],
                     start=(c == 0),
                     stop=(c == PASSES - 1),
+                )
+
+        def keep_clock(u, passes):
+            i, h = UNITS[u - 1]
+            acc[u, 0] = bank("acc", ACC_BANKS)
+            for c in range(passes):
+                cols = slice(c * P, (c + 1) * P)
+                nc.tensor.matmul_mx(
+                    out=acc[u, 0][:],
+                    lhsT=xq[i][:, cols].bitcast(FP8X4),
+                    lhsT_scale=xsc[i][:, cols],
+                    rhs=wq[c, 0][:].bitcast(FP8X4),
+                    rhs_scale=wsc[c, 0][:],
+                    start=True,
+                    stop=True,
                 )
 
         def add_item_bias(u, gl):
@@ -188,14 +213,22 @@ def tile_centred_click_probability_b15_kernel(
                 sig[u] = keep.tile([P, HALF], F32, name="sig", bufs=3)
             nc.scalar.activation(out=sig[u][:, lo:hi], in_=logit[u][:, lo:hi], func=ACT.Sigmoid, bias=user_col[:, i : i + 1])
 
-        def weigh(u, lo=0, hi=HALF):
+        def weigh(u, engine, slot, lo=0, hi=HALF):
             i, h = UNITS[u]
             if lo == 0:
                 prob[u] = keep.tile([P, HALF], F32, name="prob", bufs=4)
             nc.vector.tensor_tensor(out=prob[u][:, lo:hi], in0=sig[u][:, lo:hi], in1=exam_all[h][:, lo:hi], op=ALU.mult)
-            nc.sync.dma_start(
-                out=out_0[i * P : (i + 1) * P, h * HALF + lo : h * HALF + hi], in_=prob[u][:, lo:hi]
-            )
+
+        def store_y(u, lo=0, hi=HALF):
+            i, h = UNITS[u]
+            nc.sync.dma_start(out=out_0[i * P : (i + 1) * P, h * HALF + lo : h * HALF + hi], in_=prob[u][:, lo:hi])
+
+        def weigh_rounded(u, slot, gl):
+            i, h = UNITS[u]
+            if gl == 0:
+                pbf[u] = stage(slot)
+            cols = slice(gl * GROUP, (gl + 1) * GROUP)
+            nc.vector.tensor_tensor(out=pbf[u][:, cols], in0=sig[u][:, cols], in1=exam_all[h][:, cols], op=ALU.mult)
 
         def round_y(u, engine, slot, gls=(0, 1)):
             if gls[0] == 0:
@@ -241,11 +274,13 @@ def tile_centred_click_probability_b15_kernel(
                 scales=pscales[4 * g : P, i * P : (i + 1) * P],
                 in_=pgrp[u][:, gl * GROUP : (gl + 1) * GROUP],
             )
-            if gl == 1:
-                nc.sync.dma_start(
-                    out=words_out[:, 2 * h : 2 * h + 2, i * P : (i + 1) * P],
-                    in_=pcodes[u][:].bitcast(I32).rearrange("p (g m) -> p g m", g=2),
-                )
+
+        def store_codes(u, queue, first=0, last=2):
+            i, h = UNITS[u]
+            queue.dma_start(
+                out=words_out[:, 2 * h + first : 2 * h + last, i * P : (i + 1) * P],
+                in_=pcodes[u][:].bitcast(I32).rearrange("p (g m) -> p g m", g=2)[:, first:last, :],
+            )
 
         def spread(words, first, out, step):
             for w in range(out.shape[1] // P):
@@ -262,21 +297,14 @@ def tile_centred_click_probability_b15_kernel(
         warm = keep.tile([P, 2], F32, name="warm")
 
         def spread_mean():
-            banks = [bank("turn", TURN_BANKS), bank("turn", TURN_BANKS)]
-            spread(mean_words, 0, banks[0][:], 1)
-            spread(mean_words, 4, banks[1][:, 0:256], 1)
-            return banks
+            mean_banks[0] = bank("acc", ACC_BANKS)
+            mean_banks[1] = bank("acc", ACC_BANKS)
+            for c in range(PASSES):
+                spread(mean_words, 2 * c, mean_banks[c // 2][:, (c % 2) * 256 : (c % 2 + 1) * 256], 2)
 
-        def copy_mean(banks):
-            words = mean_all[:].bitcast(F32)
-            nc.scalar.copy(
-                out=words[:, 0:512].rearrange("p (c j w) -> p c j w", c=2, w=2),
-                in_=banks[0][:].rearrange("p (c w j) -> p c j w", c=2, w=2),
-            )
-            nc.scalar.copy(
-                out=words[:, 512:768].rearrange("p (j w) -> p j w", w=2),
-                in_=banks[1][:, 0:256].rearrange("p (w j) -> p j w", w=2),
-            )
+        def copy_mean():
+            nc.scalar.copy(out=mean_all[:, 0:HALF], in_=mean_banks[0][:].bitcast(BF16))
+            nc.scalar.copy(out=mean_all[:, HALF:K], in_=mean_banks[1][:].bitcast(BF16)[:, 0:GROUP])
 
         def spread_item(h):
             b = bank("turn", TURN_BANKS)
@@ -304,303 +332,254 @@ def tile_centred_click_probability_b15_kernel(
 
         def store_scales():
             for quad in range(4):
-                nc.sync.dma_start(
+                queue = (nc.sync, nc.scalar)[quad % 2]
+                queue.dma_start(
                     out=scales_out[:, 4 * quad : 4 * quad + 4, :],
                     in_=pscales[32 * quad : 32 * quad + 16, :].bitcast(I32),
                 )
 
-        make_identity(nc, ident_bf[:])
-        mean_words = load_row(X_mean, PASSES, "mean_row", nc.scalar)
-        nc.gpsimd.memset(user_rows[:], 0.0)
         load_xscale(0, 2, nc.scalar)
+        mean_words = load_row(X_mean, PASSES, "mean_row", nc.scalar)
         load_x(0, 1)
+        load_w(0, 0, 1)
         load_x(1, 2)
+        load_w(0, 1, 2)
+        load_w(1, 0, 2)
+        make_identity(nc, ident[:])
+        nc.gpsimd.memset(user_rows[:], 0.0)
+        make_identity(nc, ident_bf[:])
         nc.vector.memset(warm[:, 0:1], 0.0)
         nc.scalar.activation(out=warm[:, 1:2], in_=warm[:, 0:1], func=ACT.Sigmoid)
         widen_x(0, "scalar", 0, 6)
-        load_w(0, 0, 1)
-        load_w(0, 1, 2)
-        widen_x(0, "vector", 6, 12)
-        make_identity(nc, ident[:])
-        load_user()
-        item_words = load_row(item_bias, 2, "item_row", nc.sync)
-        copy_mean(spread_mean())
-        widen_x(1, "vector", 0, 6)
-        interleave_w(0, 0, "c", "vector")
-        load_w(1, 0, 2)
-        add_mean(0, "g", "vector")
+        widen_x(0, "scalar", 6, 12)
+        spread_mean()
+        widen_x(1, "scalar", 0, 6)
         widen_x(1, "scalar", 6, 12)
+        interleave_w(0, 0, "g", "vector")
+        interleave_w(0, 1, "f", "gpsimd")
+        add_mean(0, "h", "psum")
+        add_mean(1, "x0", "psum")
+        quantize_w(0, 0)
         load_w(2, 0, 2)
         turn_x(0)
-        interleave_w(0, 1, "f", "scalar")
-        group_x(0, "d", nc.scalar.copy)
-        quantize_w(0, 0)
-        exam_words = load_row(exam, 2, "exam_row", nc.sync)
-        load_xscale(2, TILES, nc.sync)
-        load_x(2, 4)
-        add_mean(1, "a", "vector")
-        interleave_w(1, 1, "i", "scalar")
+        group_x(0, "x1", nc.scalar.copy)
         turn_x(1)
-        load_w(0, 2, 4)
-        group_x(1, "c", nc.scalar.copy)
+        interleave_w(1, 0, "d", "vector")
+        interleave_w(2, 0, "c", "vector")
+        load_x(2, 4)
+        copy_mean()
+        quantize_w(1, 0)
+        interleave_w(1, 1, "i", "scalar")
         quantize_w(0, 1)
+        group_x(1, "j", nc.scalar.copy)
+        load_user()
+        item_words = load_row(item_bias, 2, "item_row", nc.sync)
+        quantize_x(1, 0)
         item0 = spread_item(0)
         quantize_x(0, 0)
-        interleave_w(2, 1, "h", "scalar")
-        turn_user()
-        load_x(4, TILES)
-        load_w(1, 2, 4)
-        load_w(2, 2, 4)
-        interleave_w(1, 0, "e", "vector")
-        copy_item(0, item0, nc.vector.tensor_copy)
-        quantize_w(1, 0)
-        quantize_w(1, 1)
-        interleave_w(2, 0, "e", "vector")
-        widen_x(3, "scalar", 0, 6)
-        widen_x(2, "scalar", 0, 6)
-        quantize_x(1, 1)
-        exam_all[0] = spread_exam(0)
-        widen_x(2, "scalar", 6, 12)
-        quantize_w(2, 0)
-        quantize_w(2, 1)
-        quantize_x(0, 1)
-        interleave_w(0, 2, "a", "vector")
-        exam_all[1] = spread_exam(1)
+        load_xscale(2, TILES, nc.sync)
         item1 = spread_item(1)
+        load_w(0, 2, 4)
+        quantize_x(1, 1)
+        quantize_w(2, 0)
+        quantize_w(1, 1)
+        quantize_x(0, 1)
+        interleave_w(2, 1, "e", "scalar")
+        turn_user()
+        widen_x(2, "vector", 0, 6)
+        quantize_w(2, 1)
         multiply(0, 0)
-        quantize_x(1, 0)
-        widen_x(3, "vector", 6, 12)
-        multiply(0, 1)
-        quantize_w(0, 2)
-        add_item_bias(0, 0)
-        interleave_w(0, 3, "d", "scalar")
         multiply(1, 0)
-        add_item_bias(0, 1)
-        sigmoid(0)
+        interleave_w(0, 2, "j", "vector")
+        load_w(1, 2, 4)
+        exam_words = load_row(exam, 2, "exam_row", nc.sync)
+        widen_x(2, "vector", 6, 12)
+        copy_item(0, item0, nc.scalar.copy)
+        interleave_w(0, 3, "f", "scalar")
+        widen_x(3, "scalar", 0, 6)
+        add_item_bias(0, 0)
+        multiply(0, 1)
         multiply(1, 1)
-        add_item_bias(1, 0)
+        add_item_bias(0, 1)
         copy_item(1, item1, nc.vector.tensor_copy)
+        load_w(2, 2, 4)
+        load_x(4, TILES)
+        add_item_bias(1, 0)
         add_item_bias(1, 1)
-        weigh(0)
-        interleave_w(1, 2, "f", "vector")
-        interleave_w(2, 2, "e", "vector")
-        add_mean(2, "a", "gpsimd")
-        quantize_w(1, 2)
-        round_y(0, "vector", "h")
-        interleave_w(1, 3, "c", "scalar")
-        quantize_w(2, 2)
+        sigmoid(0)
+        add_mean(2, "g", "gpsimd")
+        exam_all[0] = spread_exam(0)
+        interleave_w(1, 3, "x1", "scalar")
         turn_x(2)
-        quantize_w(1, 3)
-        interleave_w(2, 3, "b", "scalar")
-        multiply(2, 0)
-        quantize_w(0, 3)
-        quantize_w(2, 3)
-        widen_x(4, "scalar", 0, 6)
-        group_x(2, "f", nc.vector.tensor_copy)
-        multiply(2, 1)
-        multiply(3, 0)
+        exam_all[1] = spread_exam(1)
+        weigh(0, "vector", "a")
         sigmoid(1)
-        add_item_bias(2, 0)
-        add_mean(3, "b", "gpsimd")
-        weigh(1)
-        add_item_bias(2, 1)
-        turn_y(0)
-        round_y(1, "scalar", "i")
-        multiply(3, 1)
-        add_item_bias(3, 0)
-        add_item_bias(3, 1)
+        interleave_w(1, 2, "e", "vector")
+        interleave_w(2, 2, "c", "vector")
+        group_x(2, "a", nc.scalar.copy)
+        quantize_w(0, 2)
+        quantize_w(1, 2)
         quantize_x(2, 1)
-        sigmoid(2)
-        turn_x(3)
+        quantize_w(2, 2)
+        multiply(2, 0)
+        multiply(3, 0)
+        quantize_w(1, 3)
+        quantize_w(0, 3)
+        interleave_w(2, 3, "b", "scalar")
         quantize_x(2, 0)
-        sigmoid(3)
+        quantize_w(2, 3)
+        add_item_bias(2, 0)
+        multiply(2, 1)
+        weigh(1, "vector", "c")
+        add_item_bias(3, 0)
+        add_item_bias(2, 1)
+        widen_x(3, "scalar", 6, 12)
+        round_y(0, "scalar", "x0")
+        widen_x(4, "scalar", 0, 6)
+        multiply(3, 1)
+        turn_y(0)
+        add_item_bias(3, 1)
         multiply(4, 0)
-        group_y(0, "d", nc.vector.tensor_copy)
+        add_mean(3, "b", "gpsimd")
+        store_y(1)
         multiply(4, 1)
-        turn_y(1)
-        group_x(3, "h", nc.scalar.copy)
+        turn_x(3)
+        store_y(0)
+        round_y(1, "scalar", "d")
+        sigmoid(2)
+        sigmoid(3)
         multiply(5, 0)
+        group_y(0, "c", nc.vector.tensor_copy)
+        turn_y(1)
         widen_x(4, "vector", 6, 12)
-        add_mean(4, "x0", "gpsimd")
-        widen_x(5, "scalar", 0, 6)
-        group_y(1, "e", nc.scalar.copy)
-        weigh(2)
-        add_item_bias(4, 0)
-        multiply(5, 1)
-        add_item_bias(4, 1)
-        sigmoid(4)
-        weigh(3)
-        round_y(2, "scalar", "g", (0,))
-        widen_x(5, "scalar", 6, 12)
-        add_item_bias(5, 0)
-        add_item_bias(5, 1)
-        turn_x(4)
-        sigmoid(5)
-        group_x(4, "x0", nc.scalar.copy)
-        quantize_y(0, 0)
-        quantize_x(3, 0)
-        quantize_x(3, 1)
-        multiply(6, 0)
-        multiply(6, 1)
-        multiply(7, 0)
-        quantize_y(0, 1)
-        round_y(2, "vector", "g", (1,))
-        turn_y(2)
-        quantize_y(1, 0)
-        round_y(3, "vector", "h")
-        turn_y(3)
-        quantize_y(1, 1)
-        add_mean(5, "e", "gpsimd")
-        widen_x(6, "scalar", 0, 6)
-        group_y(2, "b", nc.scalar.copy)
-        group_y(3, "d", nc.scalar.copy)
-        weigh(4)
-        add_item_bias(6, 0)
-        multiply(7, 1)
-        add_item_bias(6, 1)
-        sigmoid(6)
-        weigh(5)
-        round_y(4, "scalar", "g", (0,))
-        widen_x(6, "scalar", 6, 12)
-        add_item_bias(7, 0)
-        add_item_bias(7, 1)
-        turn_x(5)
-        sigmoid(7)
-        group_x(5, "x1", nc.scalar.copy)
-        quantize_y(2, 0)
-        quantize_x(4, 0)
-        quantize_x(4, 1)
-        multiply(8, 0)
-        multiply(8, 1)
-        multiply(9, 0)
-        quantize_y(2, 1)
-        round_y(4, "vector", "g", (1,))
-        turn_y(4)
-        quantize_y(3, 0)
-        round_y(5, "vector", "h")
-        turn_y(5)
-        quantize_y(3, 1)
-        add_mean(6, "d", "gpsimd")
-        widen_x(7, "scalar", 0, 6)
-        group_y(4, "b", nc.scalar.copy)
-        group_y(5, "e", nc.scalar.copy)
-        weigh(6)
-        add_item_bias(8, 0)
-        multiply(9, 1)
-        add_item_bias(8, 1)
-        sigmoid(8)
-        weigh(7)
-        round_y(6, "scalar", "g", (0,))
-        widen_x(7, "scalar", 6, 12)
-        add_item_bias(9, 0)
-        add_item_bias(9, 1)
-        turn_x(6)
-        sigmoid(9)
-        group_x(6, "x0", nc.scalar.copy)
-        quantize_y(4, 0)
-        quantize_x(5, 0)
-        quantize_x(5, 1)
-        multiply(10, 0)
-        multiply(10, 1)
-        multiply(11, 0)
-        quantize_y(4, 1)
-        round_y(6, "vector", "g", (1,))
-        turn_y(6)
-        quantize_y(5, 0)
-        round_y(7, "vector", "h")
-        turn_y(7)
-        quantize_y(5, 1)
-        add_mean(7, "e", "gpsimd")
-        group_y(6, "b", nc.scalar.copy)
-        group_y(7, "d", nc.scalar.copy)
-        weigh(8)
-        add_item_bias(10, 0)
-        multiply(11, 1)
-        add_item_bias(10, 1)
-        sigmoid(10)
-        weigh(9)
-        round_y(8, "scalar", "g")
-        add_item_bias(11, 0)
-        add_item_bias(11, 1)
-        turn_x(7)
-        sigmoid(11)
-        group_x(7, "x1", nc.scalar.copy)
-        quantize_y(6, 0)
-        quantize_x(6, 0)
-        quantize_x(6, 1)
-        multiply(12, 0)
-        multiply(12, 1)
-        multiply(13, 0)
-        quantize_y(6, 1)
-        turn_y(8)
-        quantize_y(7, 0)
-        round_y(9, "vector", "h")
-        turn_y(9)
-        quantize_y(7, 1)
-        weigh(10)
+        group_x(3, "i", nc.scalar.copy)
+        last_slot = "x0"
+        for cyc in range(2, 6):
+            a = 2 * cyc
+            j = cyc + 2
+            slot = ("e", "d")[cyc % 2]
+            add_mean(j, last_slot, "gpsimd")
+            if j + 1 < TILES:
+                widen_x(j + 1, "scalar", 0, 6)
+            if cyc > 2:
+                group_y(a - 4, "b", nc.scalar.copy)
+            group_y(a - 3, slot, nc.scalar.copy)
+            weigh(a - 2, "vector", "j")
+            store_y(a - 2)
+            add_item_bias(a, 0)
+            multiply(a + 1, 1)
+            add_item_bias(a, 1)
+            sigmoid(a)
+            weigh(a - 1, "vector", "j")
+            store_y(a - 1)
+            if j + 1 < TILES:
+                round_y(a - 2, "scalar", "g", (0,))
+                widen_x(j + 1, "scalar", 6, 12)
+            else:
+                round_y(a - 2, "scalar", "g")
+            add_item_bias(a + 1, 0)
+            add_item_bias(a + 1, 1)
+            turn_x(j)
+            sigmoid(a + 1)
+            group_x(j, "x%d" % (j % 2), nc.scalar.copy)
+            quantize_y(a - 4, 0)
+            quantize_x(j - 1, 0)
+            quantize_x(j - 1, 1)
+            multiply(a + 2, 0)
+            multiply(a + 2, 1)
+            multiply(a + 3, 0)
+            quantize_y(a - 4, 1)
+            store_codes(a - 4, nc.sync)
+            if j + 1 < TILES:
+                round_y(a - 2, "vector", "g", (1,))
+            turn_y(a - 2)
+            quantize_y(a - 3, 0)
+            round_y(a - 1, "vector", "h")
+            turn_y(a - 1)
+            quantize_y(a - 3, 1)
+            store_codes(a - 3, nc.sync)
+            last_slot = slot
+
         group_y(8, "a", nc.scalar.copy)
-        group_y(9, "i", nc.scalar.copy)
+        weigh(10, "vector", "g")
         add_item_bias(12, 0)
         multiply(13, 1)
-        weigh(11)
-        round_y(10, "gpsimd", "d")
         add_item_bias(12, 1)
-        add_item_bias(13, 0)
-        quantize_y(8, 0)
-        quantize_x(7, 0)
+        weigh(11, "vector", "x1")
+        store_y(11)
         quantize_x(7, 1)
-        sigmoid(12)
-        turn_y(10)
-        multiply(14, 0)
-        quantize_y(9, 0)
-        group_y(10, "h", nc.scalar.copy)
-        add_item_bias(13, 1)
+        quantize_x(7, 0)
+        quantize_y(8, 0)
+        store_y(10)
+        add_item_bias(13, 0)
+        round_y(10, "gpsimd", "j")
         quantize_y(8, 1)
+        sigmoid(12)
+        round_y(11, "gpsimd", "a")
+        add_item_bias(13, 1)
+        weigh(12, "vector", "h")
+        multiply(14, 0)
+        group_y(9, "x0", nc.scalar.copy)
+        store_codes(8, nc.sync)
         multiply(14, 1)
-        weigh(12)
         add_item_bias(14, 0)
         sigmoid(13)
+        round_y(12, "scalar", "f")
+        multiply(15, 0)
+        quantize_y(9, 0)
+        turn_y(11)
         add_item_bias(14, 1)
         quantize_y(9, 1)
-        multiply(15, 0)
-        quantize_y(10, 0)
-        round_y(11, "gpsimd", "a")
-        weigh(13)
-        round_y(12, "scalar", "d")
+        turn_y(10)
         sigmoid(14)
-        quantize_y(10, 1)
+        store_y(12)
+        group_y(11, "x0", nc.scalar.copy)
+        weigh(13, "vector", "c")
         add_item_bias(15, 0)
-        weigh(14)
-        turn_y(11)
-        group_y(11, "b", nc.scalar.copy)
+        store_codes(9, nc.sync)
         turn_y(12)
-        group_y(12, "x0", nc.scalar.copy)
+        weigh(14, "vector", "b")
+        store_y(13)
         quantize_y(11, 0)
-        round_y(13, "scalar", "c")
-        sigmoid(15, 0, GROUP)
+        group_y(12, "c", nc.scalar.copy)
+        quantize_y(12, 0)
+        round_y(14, "vector", "x1")
+        quantize_y(11, 1)
+        group_y(10, "e", nc.scalar.copy)
+        store_y(14)
+        quantize_y(12, 1)
         multiply(15, 1)
         add_item_bias(15, 1)
-        sigmoid(15, GROUP, HALF)
-        quantize_y(12, 0)
-        quantize_y(11, 1)
-        round_y(14, "vector", "i")
-        quantize_y(12, 1)
-        turn_y(13)
-        weigh(15, 0, GROUP)
+        round_y(13, "scalar", "j")
+        quantize_y(10, 0)
+        quantize_y(10, 1)
+        sigmoid(15, 0, GROUP)
         turn_y(14)
-        group_y(13, "a", nc.scalar.copy)
-        weigh(15, GROUP, HALF)
-        round_y(15, "vector", "d", (0,))
-        group_y(14, "b", nc.vector.tensor_copy)
-        round_y(15, "scalar", "b", (1,))
-        quantize_y(13, 0)
-        quantize_y(14, 0)
-        quantize_y(13, 1)
+        turn_y(13)
+        store_codes(11, nc.sync)
+        store_codes(12, nc.sync)
+        sigmoid(15, GROUP, HALF)
+        weigh(15, "vector", "d", 0, GROUP)
+        group_y(14, "h", nc.scalar.copy)
+        round_y(15, "scalar", "b", (0,))
         turn_y(15, (0,))
+        store_codes(10, nc.sync)
+        weigh(15, "vector", "h", GROUP, HALF)
+        group_y(13, "j", nc.scalar.copy)
+        weigh_rounded(15, "x1", 1)
         turn_y(15, (1,))
-        group_y(15, "i", nc.scalar.copy, (0,))
+        quantize_y(14, 0)
         quantize_y(14, 1)
-        group_y(15, "a", nc.scalar.copy, (1,))
+        group_y(15, "d", nc.scalar.copy, (0,))
+        quantize_y(13, 0)
+        store_y(15, 0, GROUP)
+        store_y(15, GROUP, HALF)
+        quantize_y(13, 1)
         quantize_y(15, 0)
+        group_y(15, "c", nc.scalar.copy, (1,))
         quantize_y(15, 1)
+        store_codes(14, nc.sync)
+        store_codes(13, nc.sync)
+        store_codes(15, nc.sync, 0, 1)
+        store_codes(15, nc.sync, 1, 2)
         store_scales()

from contextlib import ExitStack

import concourse.mybir as mybir
from concourse.masks import make_identity

T, K, N = 1024, 1536, 2048
FLOPS = 2 * T * K * N

F32 = mybir.dt.float32
BF16 = mybir.dt.bfloat16
U32 = mybir.dt.uint32
I32 = mybir.dt.int32
U8 = mybir.dt.uint8
FP8 = mybir.dt.float8_e4m3fn
FP8X4 = mybir.dt.float8_e4m3fn_x4
ALU = mybir.AluOpType
ACT = mybir.ActivationFunctionType

P = 128
PASSES = 3
GROUP = 512
HALF = 1024
TILES = 8
BLOCK = 128
BLOCKS = 12
ACC_BANKS = 3
TURN_BANKS = 3
UNITS = [(0, 0), (1, 0), (0, 1), (1, 1)] + [(i, h) for i in range(2, TILES) for h in range(2)]


def tile_centred_click_probability_b15_kernel(
    tc, X_bytes, X_scale, X_mean, W, user_bias, item_bias, exam, out_0, out_1, out_2
):
    nc = tc.nc
    words_out = out_1.bitcast(I32).rearrange("g p m o -> p g (m o)")
    scales_out = out_2.bitcast(I32)

    with ExitStack() as ctx:
        keep = ctx.enter_context(tc.tile_pool(name="keep", bufs=1))
        psum = ctx.enter_context(tc.psum_pool(name="psum", bufs=1))
        ctx.enter_context(tc.manual_schedule())

        xbytes, xscale, wraw, wgrp, wq, wsc = {}, {}, {}, {}, {}, {}
        xwide, xsum, xturn, xgrp, xq, xsc = {}, {}, {}, {}, {}, {}
        acc, logit, sig, prob, pbf, pturn, pgrp, pcodes = {}, {}, {}, {}, {}, {}, {}, {}
        count = {"acc": 0, "turn": 0}
        exam_all, mean_banks = {}, {}

        def bank(kind, banks, dtype=F32):
            index = count[kind] % banks
            count[kind] = count[kind] + 1
            cols = GROUP if dtype == F32 else HALF
            return psum.tile([P, cols], dtype, name="%s%d" % (kind, index))

        def load_x(first, last):
            t = keep.tile([P, last - first, K], U8, name="xbytes%d" % first)
            nc.sync.dma_start(out=t[:], in_=X_bytes[first * P : last * P, :].rearrange("(i p) k -> p i k", p=P))
            for i in range(first, last):
                xbytes[i] = t[:, i - first, :]

        def load_xscale(first, last, queue):
            t = keep.tile([P, last - first, 16], F32, name="xscale%d" % first)
            queue.dma_start(
                out=t[:, :, 0:BLOCKS], in_=X_scale[first * P : last * P, :].rearrange("(i p) c -> p i c", p=P)
            )
            for i in range(first, last):
                xscale[i] = t[:, i - first, :]

        def load_w(c, first, last):
            t = keep.tile([P, 4, (last - first) * GROUP], BF16, name="wraw%d_%d" % (c, first))
            rows = W[c * GROUP : (c + 1) * GROUP, first * GROUP : last * GROUP]
            nc.sync.dma_start(out=t[:], in_=rows.rearrange("(p j) n -> p j n", j=4))
            for g in range(first, last):
                wraw[c, g] = t[:, :, (g - first) * GROUP : (g - first + 1) * GROUP]

        def load_row(row, parts, name, queue):
            t = keep.tile([P, row.shape[1] // P], BF16, name=name)
            queue.dma_start(
                out=t[:].rearrange("p (h c) -> p h c", h=parts),
                in_=row.rearrange("o (h p c) -> p (o h) c", h=parts, p=P),
            )
            return t[:].bitcast(F32)

        def stage(slot):
            return keep.tile([P, 4 * GROUP], BF16, name="stage%s" % slot, align_bytes=64)

        def interleave_w(c, g, slot, engine):
            t = stage(slot)
            dst = t[:].rearrange("p (n i j) -> p n j i", i=4, j=4)
            src = wraw[c, g].rearrange("p j (n i) -> p n j i", i=4)
            if engine == "vector":
                nc.vector.tensor_copy(out=dst, in_=src)
            elif engine == "gpsimd":
                dst = t[:].rearrange("p (n j) -> p n j", j=4)
                src = wraw[c, g].rearrange("p j n -> p n j")
                nc.gpsimd.tensor_scalar(out=dst, in0=src, scalar1=1.0, scalar2=0.0, op0=ALU.mult, op1=ALU.add)
            else:
                nc.scalar.copy(out=dst, in_=src)
            wgrp[c, g] = t

        def quantize_w(c, g):
            wq[c, g] = keep.tile([P, GROUP], U32, name="wq%d_%d" % (c, g), align_bytes=64)
            wsc[c, g] = keep.tile([P, GROUP], U8, name="wsc%d_%d" % (c, g), align_bytes=64)
            nc.vector.quantize_mx(out=wq[c, g][:].bitcast(FP8X4), scales=wsc[c, g][:], in_=wgrp[c, g][:])

        def widen_x(i, engine, first=0, last=BLOCKS):
            if first == 0:
                xwide[i] = keep.tile([P, K], F32, name="xwide", bufs=3)
            for b in range(first, last):
                cols = slice(b * BLOCK, (b + 1) * BLOCK)
                src = xbytes[i][:, cols].bitcast(FP8)
                if engine == "vector":
                    nc.vector.tensor_scalar(
                        out=xwide[i][:, cols], in0=src, scalar1=xscale[i][:, b : b + 1], scalar2=None, op0=ALU.mult
                    )
                else:
                    nc.scalar.activation(out=xwide[i][:, cols], in_=src, func=ACT.Copy, scale=xscale[i][:, b : b + 1])

        def add_mean(i, slot, engine):
            xsum[i] = stage(slot)
            if engine == "psum":
                for lo, hi in ((0, HALF), (HALF, K)):
                    nc.vector.tensor_tensor(
                        out=xsum[i][:, lo:hi],
                        in0=xwide[i][:, lo:hi],
                        in1=mean_banks[lo // HALF][:].bitcast(BF16)[:, 0 : hi - lo],
                        op=ALU.add,
                    )
                return
            add = nc.vector.tensor_tensor if engine == "vector" else nc.gpsimd.tensor_tensor
            add(out=xsum[i][:, 0:K], in0=xwide[i][:], in1=mean_all[:], op=ALU.add)

        def turn_x(i):
            words = xsum[i][:, 0:K].bitcast(F32)
            xturn[i] = [bank("turn", TURN_BANKS), bank("turn", TURN_BANKS)]
            for c in range(PASSES):
                for u in range(2):
                    slot = (2 * c + u) % 4
                    nc.tensor.transpose(
                        xturn[i][c // 2][:, slot * P : (slot + 1) * P],
                        words[:, 256 * c + u : 256 * (c + 1) : 2],
                        ident[:],
                    )

        def group_x(i, slot, copy):
            xgrp[i] = stage(slot)
            words = xgrp[i][:, 0:K].bitcast(F32)
            copy(
                out=words[:, 0:512].rearrange("p (c r u) -> p c r u", c=2, u=2),
                in_=xturn[i][0][:].rearrange("p (c u r) -> p c r u", c=2, u=2),
            )
            copy(
                out=words[:, 512:768].rearrange("p (r u) -> p r u", u=2),
                in_=xturn[i][1][:, 0:256].rearrange("p (u r) -> p r u", u=2),
            )

        def quantize_x(i, part):
            if i not in xq:
                xq[i] = keep.tile([P, PASSES * P], U32, name="xq%d" % i, align_bytes=64)
                xsc[i] = keep.tile([P, PASSES * P], U8, name="xsc%d" % i, align_bytes=64)
            lo, hi = ((0, 256), (256, 384))[part]
            nc.vector.quantize_mx(
                out=xq[i][:, lo:hi].bitcast(FP8X4), scales=xsc[i][:, lo:hi], in_=xgrp[i][:, 4 * lo : 4 * hi]
            )

        def multiply(u, gl):
            i, h = UNITS[u]
            g = 2 * h + gl
            if (u, gl) not in acc:
                acc[u, gl] = bank("acc", ACC_BANKS)
            for c in range(PASSES):
                cols = slice(c * P, (c + 1) * P)
                nc.tensor.matmul_mx(
                    out=acc[u, gl][:],
                    lhsT=xq[i][:, cols].bitcast(FP8X4),
                    lhsT_scale=xsc[i][:, cols],
                    rhs=wq[c, g][:].bitcast(FP8X4),
                    rhs_scale=wsc[c, g][:],
                    start=(c == 0),
                    stop=(c == PASSES - 1),
                )

        def keep_clock(u, passes):
            i, h = UNITS[u - 1]
            acc[u, 0] = bank("acc", ACC_BANKS)
            for c in range(passes):
                cols = slice(c * P, (c + 1) * P)
                nc.tensor.matmul_mx(
                    out=acc[u, 0][:],
                    lhsT=xq[i][:, cols].bitcast(FP8X4),
                    lhsT_scale=xsc[i][:, cols],
                    rhs=wq[c, 0][:].bitcast(FP8X4),
                    rhs_scale=wsc[c, 0][:],
                    start=True,
                    stop=True,
                )

        def add_item_bias(u, gl):
            i, h = UNITS[u]
            g = 2 * h + gl
            if gl == 0:
                logit[u] = keep.tile([P, HALF], F32, name="logit", bufs=2)
            nc.vector.tensor_tensor(
                out=logit[u][:, gl * GROUP : (gl + 1) * GROUP],
                in0=acc[u, gl][:],
                in1=item_all[:, g * GROUP : (g + 1) * GROUP],
                op=ALU.add,
            )

        def sigmoid(u, lo=0, hi=HALF):
            i, h = UNITS[u]
            if lo == 0:
                sig[u] = keep.tile([P, HALF], F32, name="sig", bufs=3)
            nc.scalar.activation(out=sig[u][:, lo:hi], in_=logit[u][:, lo:hi], func=ACT.Sigmoid, bias=user_col[:, i : i + 1])

        def weigh(u, engine, slot, lo=0, hi=HALF):
            i, h = UNITS[u]
            if lo == 0:
                prob[u] = keep.tile([P, HALF], F32, name="prob", bufs=4)
            nc.vector.tensor_tensor(out=prob[u][:, lo:hi], in0=sig[u][:, lo:hi], in1=exam_all[h][:, lo:hi], op=ALU.mult)

        def store_y(u, lo=0, hi=HALF):
            i, h = UNITS[u]
            nc.sync.dma_start(out=out_0[i * P : (i + 1) * P, h * HALF + lo : h * HALF + hi], in_=prob[u][:, lo:hi])

        def weigh_rounded(u, slot, gl):
            i, h = UNITS[u]
            if gl == 0:
                pbf[u] = stage(slot)
            cols = slice(gl * GROUP, (gl + 1) * GROUP)
            nc.vector.tensor_tensor(out=pbf[u][:, cols], in0=sig[u][:, cols], in1=exam_all[h][:, cols], op=ALU.mult)

        def round_y(u, engine, slot, gls=(0, 1)):
            if gls[0] == 0:
                pbf[u] = stage(slot)
            cols = slice(gls[0] * GROUP, (gls[-1] + 1) * GROUP)
            if engine == "vector":
                nc.vector.tensor_copy(out=pbf[u][:, cols], in_=prob[u][:, cols])
            elif engine == "gpsimd":
                nc.gpsimd.tensor_scalar(
                    out=pbf[u][:, cols], in0=prob[u][:, cols], scalar1=1.0, scalar2=0.0, op0=ALU.mult, op1=ALU.add
                )
            else:
                nc.scalar.copy(out=pbf[u][:, cols], in_=prob[u][:, cols])

        def turn_y(u, gls=(0, 1)):
            words = pbf[u][:, 0:HALF].bitcast(F32)
            pturn[u, gls[0]] = bank("turn", TURN_BANKS)
            for gl in gls:
                for half in range(2):
                    slot = 2 * gl + half
                    nc.tensor.transpose(
                        pturn[u, gls[0]][:, slot * P : (slot + 1) * P],
                        words[:, 256 * gl + half : 256 * (gl + 1) : 2],
                        ident[:],
                    )

        def group_y(u, slot, copy, gls=(0, 1)):
            if gls[0] == 0:
                pgrp[u] = stage(slot)
            cols = slice(gls[0] * 256, (gls[-1] + 1) * 256)
            copy(
                out=pgrp[u][:, 0:HALF].bitcast(F32)[:, cols].rearrange("p (g r u) -> p g r u", r=P, u=2),
                in_=pturn[u, gls[0]][:, cols].rearrange("p (g u r) -> p g r u", r=P, u=2),
            )

        def quantize_y(u, gl):
            i, h = UNITS[u]
            g = 2 * h + gl
            if gl == 0:
                pcodes[u] = keep.tile([P, 2 * P], U32, name="pcodes", bufs=3, align_bytes=64)
            nc.vector.quantize_mx(
                out=pcodes[u][:, gl * P : (gl + 1) * P].bitcast(FP8X4),
                scales=pscales[4 * g : P, i * P : (i + 1) * P],
                in_=pgrp[u][:, gl * GROUP : (gl + 1) * GROUP],
            )

        def store_codes(u, queue, first=0, last=2):
            i, h = UNITS[u]
            queue.dma_start(
                out=words_out[:, 2 * h + first : 2 * h + last, i * P : (i + 1) * P],
                in_=pcodes[u][:].bitcast(I32).rearrange("p (g m) -> p g m", g=2)[:, first:last, :],
            )

        def spread(words, first, out, step):
            for w in range(out.shape[1] // P):
                dst = out[:, w * P : (w + 1) * P] if step == 1 else out[:, w : step * P : step]
                nc.tensor.transpose(dst, words[:, first + w : first + w + 1].to_broadcast([P, P]), ident[:])

        ident = keep.tile([P, P], F32, name="ident")
        ident_bf = keep.tile([P, P], BF16, name="ident_bf")
        user_rows = keep.tile([P, P], BF16, name="user_rows")
        user_col = keep.tile([P, TILES], F32, name="user_col")
        mean_all = keep.tile([P, K], BF16, name="mean_all")
        item_all = keep.tile([P, N], BF16, name="item_all")
        pscales = keep.tile([P, T], U8, name="pscales", align_bytes=64)
        warm = keep.tile([P, 2], F32, name="warm")

        def spread_mean():
            mean_banks[0] = bank("acc", ACC_BANKS)
            mean_banks[1] = bank("acc", ACC_BANKS)
            for c in range(PASSES):
                spread(mean_words, 2 * c, mean_banks[c // 2][:, (c % 2) * 256 : (c % 2 + 1) * 256], 2)

        def copy_mean():
            nc.scalar.copy(out=mean_all[:, 0:HALF], in_=mean_banks[0][:].bitcast(BF16))
            nc.scalar.copy(out=mean_all[:, HALF:K], in_=mean_banks[1][:].bitcast(BF16)[:, 0:GROUP])

        def spread_item(h):
            b = bank("turn", TURN_BANKS)
            spread(item_words, 4 * h, b[:], 1)
            return b

        def copy_item(h, b, copy):
            copy(
                out=item_all[:].bitcast(F32)[:, h * GROUP : (h + 1) * GROUP].rearrange("p (j w) -> p j w", w=4),
                in_=b[:].rearrange("p (w j) -> p j w", w=4),
            )

        def spread_exam(h):
            b = psum.tile([P, GROUP], F32, name="exam%d" % h)
            spread(exam_words, 4 * h, b[:], 4)
            return b[:].bitcast(BF16)

        def turn_user():
            b = bank("turn", TURN_BANKS, BF16)
            nc.tensor.transpose(b[:, 0:P], user_rows[:], ident_bf[:])
            nc.scalar.copy(out=user_col[:], in_=b[:, 0:TILES])

        def load_user():
            nc.sync.dma_start(out=user_rows[0:TILES, :], in_=user_bias.rearrange("(i p) o -> i (p o)", p=P))

        def store_scales():
            for quad in range(4):
                queue = (nc.sync, nc.scalar)[quad % 2]
                queue.dma_start(
                    out=scales_out[:, 4 * quad : 4 * quad + 4, :],
                    in_=pscales[32 * quad : 32 * quad + 16, :].bitcast(I32),
                )

        load_xscale(0, 2, nc.scalar)
        mean_words = load_row(X_mean, PASSES, "mean_row", nc.scalar)
        load_x(0, 1)
        load_w(0, 0, 1)
        load_x(1, 2)
        load_w(0, 1, 2)
        load_w(1, 0, 2)
        make_identity(nc, ident[:])
        nc.gpsimd.memset(user_rows[:], 0.0)
        make_identity(nc, ident_bf[:])
        nc.vector.memset(warm[:, 0:1], 0.0)
        nc.scalar.activation(out=warm[:, 1:2], in_=warm[:, 0:1], func=ACT.Sigmoid)
        widen_x(0, "scalar", 0, 6)
        widen_x(0, "scalar", 6, 12)
        spread_mean()
        widen_x(1, "scalar", 0, 6)
        widen_x(1, "scalar", 6, 12)
        interleave_w(0, 0, "g", "vector")
        interleave_w(0, 1, "f", "gpsimd")
        add_mean(0, "h", "psum")
        add_mean(1, "x0", "psum")
        quantize_w(0, 0)
        load_w(2, 0, 2)
        turn_x(0)
        group_x(0, "x1", nc.scalar.copy)
        turn_x(1)
        interleave_w(1, 0, "d", "vector")
        interleave_w(2, 0, "c", "vector")
        load_x(2, 4)
        copy_mean()
        quantize_w(1, 0)
        interleave_w(1, 1, "i", "scalar")
        quantize_w(0, 1)
        group_x(1, "j", nc.scalar.copy)
        load_user()
        item_words = load_row(item_bias, 2, "item_row", nc.sync)
        quantize_x(1, 0)
        item0 = spread_item(0)
        quantize_x(0, 0)
        load_xscale(2, TILES, nc.sync)
        item1 = spread_item(1)
        load_w(0, 2, 4)
        quantize_x(1, 1)
        quantize_w(2, 0)
        quantize_w(1, 1)
        quantize_x(0, 1)
        interleave_w(2, 1, "e", "scalar")
        turn_user()
        widen_x(2, "vector", 0, 6)
        quantize_w(2, 1)
        multiply(0, 0)
        multiply(1, 0)
        interleave_w(0, 2, "j", "vector")
        load_w(1, 2, 4)
        exam_words = load_row(exam, 2, "exam_row", nc.sync)
        widen_x(2, "vector", 6, 12)
        copy_item(0, item0, nc.scalar.copy)
        interleave_w(0, 3, "f", "scalar")
        widen_x(3, "scalar", 0, 6)
        add_item_bias(0, 0)
        multiply(0, 1)
        multiply(1, 1)
        add_item_bias(0, 1)
        copy_item(1, item1, nc.vector.tensor_copy)
        load_w(2, 2, 4)
        load_x(4, TILES)
        add_item_bias(1, 0)
        add_item_bias(1, 1)
        sigmoid(0)
        add_mean(2, "g", "gpsimd")
        exam_all[0] = spread_exam(0)
        interleave_w(1, 3, "x1", "scalar")
        turn_x(2)
        exam_all[1] = spread_exam(1)
        weigh(0, "vector", "a")
        sigmoid(1)
        interleave_w(1, 2, "e", "vector")
        interleave_w(2, 2, "c", "vector")
        group_x(2, "a", nc.scalar.copy)
        quantize_w(0, 2)
        quantize_w(1, 2)
        quantize_x(2, 1)
        quantize_w(2, 2)
        multiply(2, 0)
        multiply(3, 0)
        quantize_w(1, 3)
        quantize_w(0, 3)
        interleave_w(2, 3, "b", "scalar")
        quantize_x(2, 0)
        quantize_w(2, 3)
        add_item_bias(2, 0)
        multiply(2, 1)
        weigh(1, "vector", "c")
        add_item_bias(3, 0)
        add_item_bias(2, 1)
        widen_x(3, "scalar", 6, 12)
        round_y(0, "scalar", "x0")
        widen_x(4, "scalar", 0, 6)
        multiply(3, 1)
        turn_y(0)
        add_item_bias(3, 1)
        multiply(4, 0)
        add_mean(3, "b", "gpsimd")
        store_y(1)
        multiply(4, 1)
        turn_x(3)
        store_y(0)
        round_y(1, "scalar", "d")
        sigmoid(2)
        sigmoid(3)
        multiply(5, 0)
        group_y(0, "c", nc.vector.tensor_copy)
        turn_y(1)
        widen_x(4, "vector", 6, 12)
        group_x(3, "i", nc.scalar.copy)
        last_slot = "x0"
        for cyc in range(2, 6):
            a = 2 * cyc
            j = cyc + 2
            slot = ("e", "d")[cyc % 2]
            add_mean(j, last_slot, "gpsimd")
            if j + 1 < TILES:
                widen_x(j + 1, "scalar", 0, 6)
            if cyc > 2:
                group_y(a - 4, "b", nc.scalar.copy)
            group_y(a - 3, slot, nc.scalar.copy)
            weigh(a - 2, "vector", "j")
            store_y(a - 2)
            add_item_bias(a, 0)
            multiply(a + 1, 1)
            add_item_bias(a, 1)
            sigmoid(a)
            weigh(a - 1, "vector", "j")
            store_y(a - 1)
            if j + 1 < TILES:
                round_y(a - 2, "scalar", "g", (0,))
                widen_x(j + 1, "scalar", 6, 12)
            else:
                round_y(a - 2, "scalar", "g")
            add_item_bias(a + 1, 0)
            add_item_bias(a + 1, 1)
            turn_x(j)
            sigmoid(a + 1)
            group_x(j, "x%d" % (j % 2), nc.scalar.copy)
            quantize_y(a - 4, 0)
            quantize_x(j - 1, 0)
            quantize_x(j - 1, 1)
            multiply(a + 2, 0)
            multiply(a + 2, 1)
            multiply(a + 3, 0)
            quantize_y(a - 4, 1)
            store_codes(a - 4, nc.sync)
            if j + 1 < TILES:
                round_y(a - 2, "vector", "g", (1,))
            turn_y(a - 2)
            quantize_y(a - 3, 0)
            round_y(a - 1, "vector", "h")
            turn_y(a - 1)
            quantize_y(a - 3, 1)
            store_codes(a - 3, nc.sync)
            last_slot = slot

        group_y(8, "a", nc.scalar.copy)
        weigh(10, "vector", "g")
        add_item_bias(12, 0)
        multiply(13, 1)
        add_item_bias(12, 1)
        weigh(11, "vector", "x1")
        store_y(11)
        quantize_x(7, 1)
        quantize_x(7, 0)
        quantize_y(8, 0)
        store_y(10)
        add_item_bias(13, 0)
        round_y(10, "gpsimd", "j")
        quantize_y(8, 1)
        sigmoid(12)
        round_y(11, "gpsimd", "a")
        add_item_bias(13, 1)
        weigh(12, "vector", "h")
        multiply(14, 0)
        group_y(9, "x0", nc.scalar.copy)
        store_codes(8, nc.sync)
        multiply(14, 1)
        add_item_bias(14, 0)
        sigmoid(13)
        round_y(12, "scalar", "f")
        multiply(15, 0)
        quantize_y(9, 0)
        turn_y(11)
        add_item_bias(14, 1)
        quantize_y(9, 1)
        turn_y(10)
        sigmoid(14)
        store_y(12)
        group_y(11, "x0", nc.scalar.copy)
        weigh(13, "vector", "c")
        add_item_bias(15, 0)
        store_codes(9, nc.sync)
        turn_y(12)
        weigh(14, "vector", "b")
        store_y(13)
        quantize_y(11, 0)
        group_y(12, "c", nc.scalar.copy)
        quantize_y(12, 0)
        round_y(14, "vector", "x1")
        quantize_y(11, 1)
        group_y(10, "e", nc.scalar.copy)
        store_y(14)
        quantize_y(12, 1)
        multiply(15, 1)
        add_item_bias(15, 1)
        round_y(13, "scalar", "j")
        quantize_y(10, 0)
        quantize_y(10, 1)
        sigmoid(15, 0, GROUP)
        turn_y(14)
        turn_y(13)
        store_codes(11, nc.sync)
        store_codes(12, nc.sync)
        sigmoid(15, GROUP, HALF)
        weigh(15, "vector", "d", 0, GROUP)
        group_y(14, "h", nc.scalar.copy)
        round_y(15, "scalar", "b", (0,))
        turn_y(15, (0,))
        store_codes(10, nc.sync)
        weigh(15, "vector", "h", GROUP, HALF)
        group_y(13, "j", nc.scalar.copy)
        weigh_rounded(15, "x1", 1)
        turn_y(15, (1,))
        quantize_y(14, 0)
        quantize_y(14, 1)
        group_y(15, "d", nc.scalar.copy, (0,))
        quantize_y(13, 0)
        store_y(15, 0, GROUP)
        store_y(15, GROUP, HALF)
        quantize_y(13, 1)
        quantize_y(15, 0)
        group_y(15, "c", nc.scalar.copy, (1,))
        quantize_y(15, 1)
        store_codes(14, nc.sync)
        store_codes(13, nc.sync)
        store_codes(15, nc.sync, 0, 1)
        store_codes(15, nc.sync, 1, 2)
        store_scales()
